import numpy as np
import ml_dtypes


def mxq(x, axis, fmt="e4m3"):
    dtype, down = {"e4m3": (ml_dtypes.float8_e4m3fn, 7), "e5m2": (ml_dtypes.float8_e5m2, 14)}[fmt]
    v = np.moveaxis(np.asarray(x, np.float32).astype(ml_dtypes.bfloat16).astype(np.float64), axis, -1)
    blocks = v.reshape(v.shape[:-1] + (-1, 32))
    amax = np.abs(blocks).max(-1, keepdims=True)
    byte = np.maximum(np.where(amax > 0, np.frexp(amax)[1] - 1 + 127, 0) - down, 1)
    scale = np.exp2(byte - 127.0)
    codes = (blocks / scale).astype(np.float32).astype(dtype).astype(np.float64)
    return np.moveaxis((codes * scale).reshape(v.shape), -1, axis)


WIDE = False


def mx_kscale(k):
    if not WIDE:
        return np.ones(k)
    levels = np.array([10, -10, 5, -5, 0])
    if k % 512:
        return np.exp2(np.random.permutation(np.resize(levels, k // 32))).repeat(32)
    a = np.empty((k // 512, 16))
    for p in range(k // 512):
        a[p, :8] = np.random.permutation(np.resize(levels, 8))
        for g in range(8):
            far = levels[np.abs(levels - a[p, g]) >= 10]
            a[p, g + 8] = far[np.random.randint(len(far))]
    return np.exp2(a.ravel()).repeat(32)


def f64(x):
    return np.asarray(x).astype(np.float64)


def striped(idx):
    return np.tile(idx.reshape(-1, 16).T, (8, 1)).astype(np.uint16)


def unstriped(offs):
    return offs[:16].T.reshape(-1).astype(np.int64)


def pack_weight(w):
    k, n = w.shape
    w = f64(np.asarray(w, np.float32).astype(ml_dtypes.bfloat16)).reshape(k // 32, 32, n)
    amax = np.abs(w).max(1)
    byte = np.clip(np.where(amax > 0, np.frexp(amax)[1] - 1 + 127 - 7, 1), 1, 254)
    scaled = (w * np.exp2(127.0 - byte)[:, None, :]).reshape(k, n).astype(np.float32)
    words = np.ascontiguousarray(scaled.reshape(k // 512, 128, 4, n).transpose(0, 1, 3, 2)).astype(ml_dtypes.float8_e4m3fn).view(np.uint8)
    return words, np.ascontiguousarray(byte.astype(np.uint8).reshape(k // 512, 16, n))


def unpack_weight(words, scales):
    g, p, n, _ = words.shape
    vals = np.ascontiguousarray(words).view(ml_dtypes.float8_e4m3fn).astype(np.float64) * np.repeat(np.exp2(scales.astype(np.float64) - 127.0), 8, axis=1)[..., None]
    return vals.transpose(0, 1, 3, 2).reshape(g * 512, n)


E2M1 = np.array([0.0, 0.5, 1.0, 1.5, 2.0, 3.0, 4.0, 6.0, -0.0, -0.5, -1.0, -1.5, -2.0, -3.0, -4.0, -6.0])


def pack_fp4(w):
    k, n = w.shape
    w = f64(np.asarray(w, np.float32).astype(ml_dtypes.bfloat16)).reshape(k // 32, 32, n)
    amax = np.abs(w).max(1)
    mant, ex = np.frexp(amax / 6.0)
    byte = np.clip(np.where(amax > 0, np.where(mant > 0.5, ex, ex - 1) + 127, 1), 1, 254)
    scaled = (w * np.exp2(127.0 - byte)[:, None, :]).reshape(k, n).astype(np.float32)
    c = np.ascontiguousarray(scaled.reshape(k // 512, 128, 4, n).transpose(0, 1, 3, 2)).astype(ml_dtypes.float4_e2m1fn).view(np.uint8) & 0xF
    words = (c[..., 0::2] | (c[..., 1::2] << 4)).reshape(k // 512, 128, 2 * n)
    return np.ascontiguousarray(words), np.ascontiguousarray(byte.astype(np.uint8).reshape(k // 512, 16, n))


def unpack_fp4(words, scales):
    g, _, n = scales.shape
    words = np.ascontiguousarray(words).reshape(g, 128, n, 2)
    nib = np.empty((g, 128, n, 4), np.uint8)
    nib[..., 0::2] = words & 0xF
    nib[..., 1::2] = words >> 4
    vals = E2M1[nib] * np.repeat(np.exp2(scales.astype(np.float64) - 127.0), 8, axis=1)[..., None]
    return vals.transpose(0, 1, 3, 2).reshape(g * 512, n)


def relu(v):
    return np.maximum(v, 0.0)


K, T, S, N, H, W = 512, 2048, 512, 128, 512, 2048


def setup_inputs():
    n = np.random.standard_normal
    s = mx_kscale(K)[:, None]
    u = mx_kscale(H)
    packed_xT = pack_weight(n((K, T)) * s)
    packed_eT = pack_weight(n((K, W)) * s)
    packed_w2 = pack_fp4(n((H, N)) / np.sqrt(H) / u[:, None])
    return {
        "x_words": packed_xT[0],
        "x_scales": packed_xT[1],
        "e_words": packed_eT[0],
        "e_scales": packed_eT[1],
        "w1": (n((K, H)) / np.sqrt(K) / s * u).astype(np.float32),
        "w2_words": packed_w2[0],
        "w2_scales": packed_w2[1],
        "w3": (n((K, N)) / np.sqrt(K) / s).astype(np.float32),
        "offs": striped(np.random.permutation(T)[:S]),
        "fea": striped(np.random.permutation(W)[:S]),
    }


def reference(x_words, x_scales, e_words, e_scales, w1, w2_words, w2_scales, w3, offs, fea):
    e_fea = unpack_weight(e_words, e_scales)[:, unstriped(fea)]
    fval = mxq(f64(w3), 0, "e4m3").T @ e_fea
    mu = fval.mean(axis=1, keepdims=True)
    dv = fval - mu
    dv2 = (dv) ** 2
    sd = np.sqrt(dv2.mean(axis=1, keepdims=True) + 0.05)
    xq = unpack_weight(x_words, x_scales)[:, unstriped(offs)]
    h = relu(mxq(f64(w1), 0, "e4m3").T @ xq)
    mask = unpack_fp4(w2_words, w2_scales).T @ mxq(h, 0, "e4m3")
    return np.tanh((dv / sd) * mask) + 0.3 * mask

@@ -1,0 +1,180 @@
+from contextlib import ExitStack
+
+import concourse.mybir as mybir
+
+K, T, S, N, H = 512, 2048, 512, 128, 512
+FLOPS = 2 * K * S * N + 2 * K * S * H + 2 * H * S * N
+
+F32 = mybir.dt.float32
+BF16 = mybir.dt.bfloat16
+I32 = mybir.dt.int32
+U32 = mybir.dt.uint32
+U16 = mybir.dt.uint16
+U8 = mybir.dt.uint8
+FP8X4 = mybir.dt.float8_e4m3fn_x4
+FP4X4 = mybir.dt.float4_e2m1fn_x4
+ALU = mybir.AluOpType
+ACT = mybir.ActivationFunctionType
+
+P = 128
+PACK = 4
+HALF = S // 2
+CHUNK = 128
+X_ROW = 4
+E_ROW = 8
+EPS = 0.05
+MASK_SHARE = 0.3
+
+
+def load_scale_rows(queue, plane, scales, first_row):
+    rows = scales[0].bitcast(I32)
+    for r in range(4):
+        queue.dma_start(out=plane[:].bitcast(I32)[first_row + r : P : 32, :], in_=rows[r:16:4, :])
+
+
+def tile_picked_ymaskn_tanh_p_kernel(
+    tc, x_words, x_scales, e_words, e_scales, w1, w2_words, w2_scales, w3, offs, fea, out
+):
+    nc = tc.nc
+    with ExitStack() as ctx:
+        lists = ctx.enter_context(tc.tile_pool(name="lists", bufs=1))
+        sb = ctx.enter_context(tc.tile_pool(name="sb", bufs=1))
+        psum = ctx.enter_context(tc.psum_pool(name="psum", bufs=1))
+
+        offs_sb = lists.tile([P, S // 16], U16, name="offs_sb")
+        fea_sb = lists.tile([P, S // 16], U16, name="fea_sb")
+        x_plane = sb.tile([P, T], U8, name="x_plane")
+        e_plane = sb.tile([P, T], U8, name="e_plane")
+        w2_plane = sb.tile([P, N], U8, name="w2_plane", align_bytes=64)
+        w2_codes = sb.tile([P, 2 * N], U8, name="w2_codes", align_bytes=64)
+        x_table = sb.tile([P, T], U32, name="x_table")
+        e_table = sb.tile([P, T], U32, name="e_table")
+        w1_raw = [sb.tile([P, PACK, H // 2], F32, name="w1_raw%d" % c) for c in range(2)]
+        w3_raw = sb.tile([P, PACK, N], F32, name="w3_raw")
+        power = sb.tile([P, 1], F32, name="power")
+
+        nc.vector.memset(x_plane[:].bitcast(I32), 0)
+        nc.vector.memset(e_plane[:].bitcast(I32), 0)
+        nc.gpsimd.memset(w2_plane[:].bitcast(I32), 0)
+        nc.gpsimd.memset(power[:], -0.5)
+
+        w1_rows = w1.rearrange("(p j) c -> p j c", j=PACK)
+        nc.sync.dma_start(offs_sb[:], offs)
+        nc.sync.dma_start(fea_sb[:], fea)
+        for c in range(2):
+            nc.sync.dma_start(out=w1_raw[c][:], in_=w1_rows[:, :, c * H // 2 : (c + 1) * H // 2])
+        load_scale_rows(nc.sync, x_plane, x_scales, X_ROW)
+        nc.sync.dma_start(out=x_table[:].bitcast(I32), in_=x_words[0].rearrange("p n t -> p (n t)").bitcast(I32))
+        load_scale_rows(nc.sync, e_plane, e_scales, E_ROW)
+        nc.sync.dma_start(out=w3_raw[:], in_=w3.rearrange("(p j) c -> p j c", j=PACK))
+        nc.sync.dma_start(out=e_table[:].bitcast(I32), in_=e_words[0].rearrange("p n t -> p (n t)").bitcast(I32))
+        nc.gpsimd.dma_start(out=w2_codes[:].bitcast(I32), in_=w2_words[0].bitcast(I32))
+        load_scale_rows(nc.gpsimd, w2_plane, w2_scales, 0)
+
+        w1_bf = sb.tile([P, PACK, P, PACK], BF16, name="w1_bf", align_bytes=64)
+        for c in range(2):
+            nc.scalar.activation(
+                out=w1_bf[:, :, c * P // 2 : (c + 1) * P // 2, :].rearrange("p t m j -> p m t j"),
+                in_=w1_raw[c][:].rearrange("p j (m t) -> p m t j", t=PACK),
+                func=ACT.Copy,
+            )
+        x_bytes = sb.tile([P, S], U8, name="x_bytes", align_bytes=64)
+        nc.vector.tensor_copy(x_bytes[:], x_plane[:].indirect(offs_sb[:]))
+        w1_codes = sb.tile([P, H], U32, name="w1_codes", align_bytes=64)
+        w1_bytes = sb.tile([P, H], U8, name="w1_bytes", align_bytes=64)
+        nc.vector.quantize_mx(
+            out=w1_codes[:].bitcast(FP8X4), scales=w1_bytes[:], in_=w1_bf[:].rearrange("p t m j -> p (t m j)")
+        )
+        e_bytes = sb.tile([P, S], U8, name="e_bytes", align_bytes=64)
+        nc.vector.tensor_copy(e_bytes[:], e_plane[:].indirect(fea_sb[:]))
+
+        x_codes = [sb.tile([P, HALF], U32, name="x_codes%d" % h, align_bytes=64) for h in range(2)]
+        for h in range(2):
+            nc.vector.tensor_copy(x_codes[h][:], x_table[:].indirect(offs_sb[:, h * HALF // 16 : (h + 1) * HALF // 16]))
+
+        w3_bf = sb.tile([P, N, PACK], BF16, name="w3_bf", align_bytes=64)
+        nc.scalar.activation(
+            out=w3_bf[:].rearrange("p (c i) j -> p c j i", i=4),
+            in_=w3_raw[:].rearrange("p j (c i) -> p c j i", i=4),
+            func=ACT.Copy,
+        )
+        w3_codes = sb.tile([P, N], U32, name="w3_codes", align_bytes=64)
+        w3_bytes = sb.tile([P, N], U8, name="w3_bytes", align_bytes=64)
+        nc.vector.quantize_mx(
+            out=w3_codes[:].bitcast(FP8X4), scales=w3_bytes[:], in_=w3_bf[:].rearrange("p c j -> p (c j)")
+        )
+
+        h_bf = [sb.tile([P, HALF, PACK], BF16, name="h_bf%d" % h, align_bytes=64) for h in range(2)]
+        for chunk in range(S // CHUNK):
+            h, c = divmod(chunk, HALF // CHUNK)
+            bank = psum.tile([P, PACK, CHUNK], F32, name="h_bank%d" % chunk)
+            for t in range(PACK):
+                nc.tensor.matmul_mx(
+                    out=bank[:, t, :],
+                    lhsT=w1_codes[:, t * P : (t + 1) * P].bitcast(FP8X4),
+                    lhsT_scale=w1_bytes[:, t * P : (t + 1) * P],
+                    rhs=x_codes[h][:, c * CHUNK : (c + 1) * CHUNK].bitcast(FP8X4),
+                    rhs_scale=x_bytes[X_ROW:P, chunk * CHUNK : (chunk + 1) * CHUNK],
+                    start=True,
+                    stop=True,
+                )
+            woven = h_bf[h][:, c * CHUNK : (c + 1) * CHUNK, :]
+            if chunk == 1:
+                nc.vector.tensor_scalar_max(out=woven, in0=bank[:].rearrange("p t n -> p n t"), scalar1=0.0)
+            else:
+                nc.scalar.activation(out=woven, in_=bank[:].rearrange("p t n -> p n t"), func=ACT.Relu)
+
+        mask_part = [sb.tile([P, HALF], F32, name="mask_part%d" % h) for h in range(2)]
+        e_codes = [sb.tile([P, HALF], U32, name="e_codes%d" % h, align_bytes=64) for h in range(2)]
+        f_banks = [psum.tile([P, HALF], F32, name="f_bank%d" % h) for h in range(2)]
+        stats = sb.tile([P, 2, 6], F32, name="stats")
+        for h in range(2):
+            h_codes = sb.tile([P, HALF], U32, name="h_codes%d" % h, align_bytes=64)
+            h_bytes = sb.tile([P, HALF], U8, name="h_bytes%d" % h, align_bytes=64)
+            nc.vector.quantize_mx(
+                out=h_codes[:].bitcast(FP8X4), scales=h_bytes[:], in_=h_bf[h][:].rearrange("p n t -> p (n t)")
+            )
+            mask_bank = psum.tile([P, HALF], F32, name="mask_bank%d" % h)
+            nc.tensor.matmul_mx(
+                out=mask_bank[:],
+                lhsT=w2_codes[:].bitcast(FP4X4),
+                lhsT_scale=w2_plane[:],
+                rhs=h_codes[:].bitcast(FP8X4),
+                rhs_scale=h_bytes[:],
+                start=True,
+                stop=True,
+            )
+            nc.scalar.activation(out=mask_part[h][:], in_=mask_bank[:], func=ACT.Copy, scale=MASK_SHARE)
+            nc.vector.tensor_copy(e_codes[h][:], e_table[:].indirect(fea_sb[:, h * HALF // 16 : (h + 1) * HALF // 16]))
+            nc.tensor.matmul_mx(
+                out=f_banks[h][:],
+                lhsT=w3_codes[:].bitcast(FP8X4),
+                lhsT_scale=w3_bytes[:],
+                rhs=e_codes[h][:].bitcast(FP8X4),
+                rhs_scale=e_bytes[E_ROW:P, h * HALF : (h + 1) * HALF],
+                start=True,
+                stop=True,
+            )
+        for h in range(2):
+            nc.vector.bn_stats(out=stats[:, h, :], in_=f_banks[h][:])
+        moments = sb.tile([P, 2], F32, name="moments")
+        nc.vector.bn_aggr(out=moments[:], in_=stats[:].rearrange("p h s -> p (h s)"))
+        scaled_var = sb.tile([P, 1], F32, name="scaled_var")
+        gain = sb.tile([P, 1], F32, name="gain")
+        nc.gpsimd.tensor_scalar(
+            out=scaled_var[:], in0=moments[:, 1:2], scalar1=EPS, scalar2=MASK_SHARE * MASK_SHARE, op0=ALU.add, op1=ALU.mult
+        )
+        nc.gpsimd.tensor_tensor(out=gain[:], in0=scaled_var[:], in1=power[:], op=ALU.pow)
+
+        prod = [sb.tile([P, HALF], F32, name="prod%d" % h) for h in range(2)]
+        bounded = [sb.tile([P, HALF], F32, name="bounded%d" % h) for h in range(2)]
+        result = [sb.tile([P, HALF], F32, name="result%d" % h) for h in range(2)]
+        for h in range(2):
+            nc.vector.scalar_tensor_tensor(
+                out=prod[h][:], in0=f_banks[h][:], scalar=moments[:, 0:1], in1=mask_part[h][:],
+                op0=ALU.subtract, op1=ALU.mult,
+            )
+            nc.scalar.activation(out=bounded[h][:], in_=prod[h][:], func=ACT.Tanh, scale=gain[:])
+        for h in range(2):
+            nc.vector.tensor_tensor(out=result[h][:], in0=bounded[h][:], in1=mask_part[h][:], op=ALU.add)
+            nc.sync.dma_start(out=out[:, h * HALF : (h + 1) * HALF], in_=result[h][:])

@@ -44,40 +44,38 @@ def tile_picked_ymaskn_tanh_p_kernel(
         offs_sb = lists.tile([P, S // 16], U16, name="offs_sb")
         fea_sb = lists.tile([P, S // 16], U16, name="fea_sb")
         x_plane = sb.tile([P, T], U8, name="x_plane")
-        e_plane = sb.tile([P, T], U8, name="e_plane")
+        e_plane = sb.tile([P, T], U8, name="e_plane", tag="h_bytes0", align_bytes=64)
         w2_plane = sb.tile([P, N], U8, name="w2_plane", align_bytes=64)
         w2_codes = sb.tile([P, 2 * N], U8, name="w2_codes", align_bytes=64)
         x_table = sb.tile([P, T], U32, name="x_table")
-        e_table = sb.tile([P, T], U32, name="e_table")
+        e_table = sb.tile([P, T], U32, name="e_table", tag="h_codes1", align_bytes=64)
         w1_raw = [sb.tile([P, PACK, H // 2], F32, name="w1_raw%d" % c) for c in range(2)]
-        w3_raw = sb.tile([P, PACK, N], F32, name="w3_raw")
+        w3_raw = sb.tile([P, PACK, N], F32, name="w3_raw", tag="h_bf0", align_bytes=64)
         power = sb.tile([P, 1], F32, name="power")
 
         nc.vector.memset(x_plane[:].bitcast(I32), 0)
         nc.vector.memset(e_plane[:].bitcast(I32), 0)
-        nc.gpsimd.memset(w2_plane[:].bitcast(I32), 0)
-        nc.gpsimd.memset(power[:], -0.5)
+        nc.vector.memset(w2_plane[:].bitcast(I32), 0)
+        nc.vector.memset(power[:], -0.5)
 
         w1_rows = w1.rearrange("(p j) c -> p j c", j=PACK)
         nc.sync.dma_start(offs_sb[:], offs)
-        nc.sync.dma_start(fea_sb[:], fea)
         for c in range(2):
             nc.sync.dma_start(out=w1_raw[c][:], in_=w1_rows[:, :, c * H // 2 : (c + 1) * H // 2])
         load_scale_rows(nc.sync, x_plane, x_scales, X_ROW)
         nc.sync.dma_start(out=x_table[:].bitcast(I32), in_=x_words[0].rearrange("p n t -> p (n t)").bitcast(I32))
-        load_scale_rows(nc.sync, e_plane, e_scales, E_ROW)
+        nc.sync.dma_start(fea_sb[:], fea)
         nc.sync.dma_start(out=w3_raw[:], in_=w3.rearrange("(p j) c -> p j c", j=PACK))
+        load_scale_rows(nc.sync, e_plane, e_scales, E_ROW)
         nc.sync.dma_start(out=e_table[:].bitcast(I32), in_=e_words[0].rearrange("p n t -> p (n t)").bitcast(I32))
-        nc.gpsimd.dma_start(out=w2_codes[:].bitcast(I32), in_=w2_words[0].bitcast(I32))
-        load_scale_rows(nc.gpsimd, w2_plane, w2_scales, 0)
+        nc.sync.dma_start(out=w2_codes[:].bitcast(I32), in_=w2_words[0].bitcast(I32))
+        load_scale_rows(nc.sync, w2_plane, w2_scales, 0)
 
         w1_bf = sb.tile([P, PACK, P, PACK], BF16, name="w1_bf", align_bytes=64)
-        for c in range(2):
-            nc.scalar.activation(
-                out=w1_bf[:, :, c * P // 2 : (c + 1) * P // 2, :].rearrange("p t m j -> p m t j"),
-                in_=w1_raw[c][:].rearrange("p j (m t) -> p m t j", t=PACK),
-                func=ACT.Copy,
-            )
+        dealt = [w1_bf[:, :, c * P // 2 : (c + 1) * P // 2, :].rearrange("p t m j -> p m t j") for c in range(2)]
+        plain = [w1_raw[c][:].rearrange("p j (m t) -> p m t j", t=PACK) for c in range(2)]
+        nc.vector.tensor_copy(out=dealt[0], in_=plain[0])
+        nc.scalar.activation(out=dealt[1], in_=plain[1], func=ACT.Copy)
         x_bytes = sb.tile([P, S], U8, name="x_bytes", align_bytes=64)
         nc.vector.tensor_copy(x_bytes[:], x_plane[:].indirect(offs_sb[:]))
         w1_codes = sb.tile([P, H], U32, name="w1_codes", align_bytes=64)
@@ -85,14 +83,14 @@ def tile_picked_ymaskn_tanh_p_kernel(
         nc.vector.quantize_mx(
             out=w1_codes[:].bitcast(FP8X4), scales=w1_bytes[:], in_=w1_bf[:].rearrange("p t m j -> p (t m j)")
         )
-        e_bytes = sb.tile([P, S], U8, name="e_bytes", align_bytes=64)
-        nc.vector.tensor_copy(e_bytes[:], e_plane[:].indirect(fea_sb[:]))
 
         x_codes = [sb.tile([P, HALF], U32, name="x_codes%d" % h, align_bytes=64) for h in range(2)]
         for h in range(2):
             nc.vector.tensor_copy(x_codes[h][:], x_table[:].indirect(offs_sb[:, h * HALF // 16 : (h + 1) * HALF // 16]))
 
-        w3_bf = sb.tile([P, N, PACK], BF16, name="w3_bf", align_bytes=64)
+        e_bytes = sb.tile([P, S], U8, name="e_bytes", align_bytes=64)
+        nc.vector.tensor_copy(e_bytes[:], e_plane[:].indirect(fea_sb[:]))
+        w3_bf = sb.tile([P, N, PACK], BF16, name="w3_bf", tag="h_codes0", align_bytes=64)
         nc.scalar.activation(
             out=w3_bf[:].rearrange("p (c i) j -> p c j i", i=4),
             in_=w3_raw[:].rearrange("p j (c i) -> p c j i", i=4),
@@ -104,7 +102,7 @@ def tile_picked_ymaskn_tanh_p_kernel(
             out=w3_codes[:].bitcast(FP8X4), scales=w3_bytes[:], in_=w3_bf[:].rearrange("p c j -> p (c j)")
         )
 
-        h_bf = [sb.tile([P, HALF, PACK], BF16, name="h_bf%d" % h, align_bytes=64) for h in range(2)]
+        h_bf = sb.tile([P, S, PACK], BF16, name="h_bf", tag="h_bf0", align_bytes=64)
         for chunk in range(S // CHUNK):
             h, c = divmod(chunk, HALF // CHUNK)
             bank = psum.tile([P, PACK, CHUNK], F32, name="h_bank%d" % chunk)
@@ -118,21 +116,19 @@ def tile_picked_ymaskn_tanh_p_kernel(
                     start=True,
                     stop=True,
                 )
-            woven = h_bf[h][:, c * CHUNK : (c + 1) * CHUNK, :]
-            if chunk == 1:
-                nc.vector.tensor_scalar_max(out=woven, in0=bank[:].rearrange("p t n -> p n t"), scalar1=0.0)
-            else:
-                nc.scalar.activation(out=woven, in_=bank[:].rearrange("p t n -> p n t"), func=ACT.Relu)
+            woven = h_bf[:, chunk * CHUNK : (chunk + 1) * CHUNK, :]
+            nc.scalar.activation(out=woven, in_=bank[:].rearrange("p t n -> p n t"), func=ACT.Relu)
 
         mask_part = [sb.tile([P, HALF], F32, name="mask_part%d" % h) for h in range(2)]
         e_codes = [sb.tile([P, HALF], U32, name="e_codes%d" % h, align_bytes=64) for h in range(2)]
         f_banks = [psum.tile([P, HALF], F32, name="f_bank%d" % h) for h in range(2)]
         stats = sb.tile([P, 2, 6], F32, name="stats")
-        for h in range(2):
-            h_codes = sb.tile([P, HALF], U32, name="h_codes%d" % h, align_bytes=64)
-            h_bytes = sb.tile([P, HALF], U8, name="h_bytes%d" % h, align_bytes=64)
+
+        def mask_half(h):
+            h_codes = sb.tile([P, HALF], U32, name="h_codes%d" % h, tag="h_codes%d" % h, align_bytes=64)
+            h_bytes = sb.tile([P, HALF], U8, name="h_bytes%d" % h, tag="h_bytes%d" % h, align_bytes=64)
             nc.vector.quantize_mx(
-                out=h_codes[:].bitcast(FP8X4), scales=h_bytes[:], in_=h_bf[h][:].rearrange("p n t -> p (n t)")
+                out=h_codes[:].bitcast(FP8X4), scales=h_bytes[:], in_=h_bf[:, h * HALF : (h + 1) * HALF, :].rearrange("p n t -> p (n t)")
             )
             mask_bank = psum.tile([P, HALF], F32, name="mask_bank%d" % h)
             nc.tensor.matmul_mx(
@@ -145,6 +141,8 @@ def tile_picked_ymaskn_tanh_p_kernel(
                 stop=True,
             )
             nc.scalar.activation(out=mask_part[h][:], in_=mask_bank[:], func=ACT.Copy, scale=MASK_SHARE)
+
+        def feature_half(h):
             nc.vector.tensor_copy(e_codes[h][:], e_table[:].indirect(fea_sb[:, h * HALF // 16 : (h + 1) * HALF // 16]))
             nc.tensor.matmul_mx(
                 out=f_banks[h][:],
@@ -155,6 +153,11 @@ def tile_picked_ymaskn_tanh_p_kernel(
                 start=True,
                 stop=True,
             )
+
+        mask_half(0)
+        feature_half(0)
+        feature_half(1)
+        mask_half(1)
         for h in range(2):
             nc.vector.bn_stats(out=stats[:, h, :], in_=f_banks[h][:])
         moments = sb.tile([P, 2], F32, name="moments")

@@ -44,11 +44,11 @@ def tile_picked_ymaskn_tanh_p_kernel(
         offs_sb = lists.tile([P, S // 16], U16, name="offs_sb")
         fea_sb = lists.tile([P, S // 16], U16, name="fea_sb")
         x_plane = sb.tile([P, T], U8, name="x_plane")
-        e_plane = sb.tile([P, T], U8, name="e_plane", tag="h_bytes0", align_bytes=64)
+        e_plane = sb.tile([P, T], U8, name="e_plane", tag="w3_codes", align_bytes=64)
         w2_plane = sb.tile([P, N], U8, name="w2_plane", align_bytes=64)
         w2_codes = sb.tile([P, 2 * N], U8, name="w2_codes", align_bytes=64)
         x_table = sb.tile([P, T], U32, name="x_table")
-        e_table = sb.tile([P, T], U32, name="e_table", tag="h_codes1", align_bytes=64)
+        e_table = sb.tile([P, T], U32, name="e_table", tag="h_codes", align_bytes=64)
         w1_raw = [sb.tile([P, PACK, H // 2], F32, name="w1_raw%d" % c) for c in range(2)]
         w3_raw = sb.tile([P, PACK, N], F32, name="w3_raw", tag="h_bf0", align_bytes=64)
         power = sb.tile([P, 1], F32, name="power")
@@ -90,13 +90,13 @@ def tile_picked_ymaskn_tanh_p_kernel(
 
         e_bytes = sb.tile([P, S], U8, name="e_bytes", align_bytes=64)
         nc.vector.tensor_copy(e_bytes[:], e_plane[:].indirect(fea_sb[:]))
-        w3_bf = sb.tile([P, N, PACK], BF16, name="w3_bf", tag="h_codes0", align_bytes=64)
+        w3_bf = sb.tile([P, N, PACK], BF16, name="w3_bf", align_bytes=64)
         nc.scalar.activation(
             out=w3_bf[:].rearrange("p (c i) j -> p c j i", i=4),
             in_=w3_raw[:].rearrange("p j (c i) -> p c j i", i=4),
             func=ACT.Copy,
         )
-        w3_codes = sb.tile([P, N], U32, name="w3_codes", align_bytes=64)
+        w3_codes = sb.tile([P, N], U32, name="w3_codes", tag="w3_codes", align_bytes=64)
         w3_bytes = sb.tile([P, N], U8, name="w3_bytes", align_bytes=64)
         nc.vector.quantize_mx(
             out=w3_codes[:].bitcast(FP8X4), scales=w3_bytes[:], in_=w3_bf[:].rearrange("p c j -> p (c j)")
@@ -119,30 +119,10 @@ def tile_picked_ymaskn_tanh_p_kernel(
             woven = h_bf[:, chunk * CHUNK : (chunk + 1) * CHUNK, :]
             nc.scalar.activation(out=woven, in_=bank[:].rearrange("p t n -> p n t"), func=ACT.Relu)
 
-        mask_part = [sb.tile([P, HALF], F32, name="mask_part%d" % h) for h in range(2)]
         e_codes = [sb.tile([P, HALF], U32, name="e_codes%d" % h, align_bytes=64) for h in range(2)]
         f_banks = [psum.tile([P, HALF], F32, name="f_bank%d" % h) for h in range(2)]
-        stats = sb.tile([P, 2, 6], F32, name="stats")
-
-        def mask_half(h):
-            h_codes = sb.tile([P, HALF], U32, name="h_codes%d" % h, tag="h_codes%d" % h, align_bytes=64)
-            h_bytes = sb.tile([P, HALF], U8, name="h_bytes%d" % h, tag="h_bytes%d" % h, align_bytes=64)
-            nc.vector.quantize_mx(
-                out=h_codes[:].bitcast(FP8X4), scales=h_bytes[:], in_=h_bf[:, h * HALF : (h + 1) * HALF, :].rearrange("p n t -> p (n t)")
-            )
-            mask_bank = psum.tile([P, HALF], F32, name="mask_bank%d" % h)
-            nc.tensor.matmul_mx(
-                out=mask_bank[:],
-                lhsT=w2_codes[:].bitcast(FP4X4),
-                lhsT_scale=w2_plane[:],
-                rhs=h_codes[:].bitcast(FP8X4),
-                rhs_scale=h_bytes[:],
-                start=True,
-                stop=True,
-            )
-            nc.scalar.activation(out=mask_part[h][:], in_=mask_bank[:], func=ACT.Copy, scale=MASK_SHARE)
-
-        def feature_half(h):
+        mask_banks = [psum.tile([P, HALF], F32, name="mask_bank%d" % h) for h in range(2)]
+        for h in range(2):
             nc.vector.tensor_copy(e_codes[h][:], e_table[:].indirect(fea_sb[:, h * HALF // 16 : (h + 1) * HALF // 16]))
             nc.tensor.matmul_mx(
                 out=f_banks[h][:],
@@ -153,31 +133,54 @@ def tile_picked_ymaskn_tanh_p_kernel(
                 start=True,
                 stop=True,
             )
-
-        mask_half(0)
-        feature_half(0)
-        feature_half(1)
-        mask_half(1)
-        for h in range(2):
-            nc.vector.bn_stats(out=stats[:, h, :], in_=f_banks[h][:])
-        moments = sb.tile([P, 2], F32, name="moments")
-        nc.vector.bn_aggr(out=moments[:], in_=stats[:].rearrange("p h s -> p (h s)"))
-        scaled_var = sb.tile([P, 1], F32, name="scaled_var")
-        gain = sb.tile([P, 1], F32, name="gain")
-        nc.gpsimd.tensor_scalar(
-            out=scaled_var[:], in0=moments[:, 1:2], scalar1=EPS, scalar2=MASK_SHARE * MASK_SHARE, op0=ALU.add, op1=ALU.mult
+        h_codes = sb.tile([P, S], U32, name="h_codes", tag="h_codes", align_bytes=64)
+        h_bytes = sb.tile([P, S], U8, name="h_bytes", align_bytes=64)
+        nc.vector.quantize_mx(
+            out=h_codes[:].bitcast(FP8X4), scales=h_bytes[:], in_=h_bf[:].rearrange("p n t -> p (n t)")
         )
-        nc.gpsimd.tensor_tensor(out=gain[:], in0=scaled_var[:], in1=power[:], op=ALU.pow)
+        for h in range(2):
+            nc.tensor.matmul_mx(
+                out=mask_banks[h][:],
+                lhsT=w2_codes[:].bitcast(FP4X4),
+                lhsT_scale=w2_plane[:],
+                rhs=h_codes[:, h * HALF : (h + 1) * HALF].bitcast(FP8X4),
+                rhs_scale=h_bytes[:, h * HALF : (h + 1) * HALF],
+                start=True,
+                stop=True,
+            )
 
+        stats = sb.tile([P, 9], F32, name="stats")
+        sums = sb.tile([P, 2], F32, name="sums")
+        f_first = sb.tile([P, HALF], F32, name="f_first")
+        squares = sb.tile([P, HALF], F32, name="squares")
+        nc.vector.memset(stats[:, 0:1], float(HALF))
+        nc.scalar.activation(out=f_first[:], in_=f_banks[0][:], func=ACT.Copy, accum_out=sums[:, 0:1])
+        nc.scalar.activation(out=stats[:, 1:2], in_=sums[:, 0:1], func=ACT.Copy, scale=1.0 / HALF)
+        nc.scalar.activation(
+            out=squares[:], in_=f_first[:], func=ACT.Square, scale=-1.0, bias=stats[:, 1:2], accum_out=sums[:, 1:2]
+        )
+        nc.scalar.activation(out=stats[:, 2:3], in_=sums[:, 1:2], func=ACT.Copy, bias=EPS * S)
+        nc.vector.bn_stats(out=stats[:, 3:9], in_=f_banks[1][:])
+        moments = sb.tile([P, 2], F32, name="moments")
+        nc.vector.bn_aggr(out=moments[:], in_=stats[:])
+        gain = sb.tile([P, 1], F32, name="gain")
+        nc.gpsimd.tensor_tensor(out=gain[:], in0=moments[:, 1:2], in1=power[:], op=ALU.pow)
+
+        mask_second = sb.tile([P, HALF], F32, name="mask_second")
+        nc.scalar.activation(out=mask_second[:], in_=mask_banks[1][:], func=ACT.Copy)
+        factors = [(f_first, mask_banks[0]), (f_banks[1], mask_second)]
         prod = [sb.tile([P, HALF], F32, name="prod%d" % h) for h in range(2)]
         bounded = [sb.tile([P, HALF], F32, name="bounded%d" % h) for h in range(2)]
         result = [sb.tile([P, HALF], F32, name="result%d" % h) for h in range(2)]
         for h in range(2):
             nc.vector.scalar_tensor_tensor(
-                out=prod[h][:], in0=f_banks[h][:], scalar=moments[:, 0:1], in1=mask_part[h][:],
+                out=prod[h][:], in0=factors[h][0][:], scalar=moments[:, 0:1], in1=factors[h][1][:],
                 op0=ALU.subtract, op1=ALU.mult,
             )
             nc.scalar.activation(out=bounded[h][:], in_=prod[h][:], func=ACT.Tanh, scale=gain[:])
         for h in range(2):
-            nc.vector.tensor_tensor(out=result[h][:], in0=bounded[h][:], in1=mask_part[h][:], op=ALU.add)
+            nc.vector.scalar_tensor_tensor(
+                out=result[h][:], in0=mask_banks[h][:], scalar=MASK_SHARE, in1=bounded[h][:],
+                op0=ALU.mult, op1=ALU.add,
+            )
             nc.sync.dma_start(out=out[:, h * HALF : (h + 1) * HALF], in_=result[h][:])

from contextlib import ExitStack

import concourse.mybir as mybir

K, T, S, N, H = 512, 2048, 512, 128, 512
FLOPS = 2 * K * S * N + 2 * K * S * H + 2 * H * S * N

F32 = mybir.dt.float32
BF16 = mybir.dt.bfloat16
I32 = mybir.dt.int32
U32 = mybir.dt.uint32
U16 = mybir.dt.uint16
U8 = mybir.dt.uint8
FP8X4 = mybir.dt.float8_e4m3fn_x4
FP4X4 = mybir.dt.float4_e2m1fn_x4
ALU = mybir.AluOpType
ACT = mybir.ActivationFunctionType

P = 128
PACK = 4
HALF = S // 2
CHUNK = 128
X_ROW = 4
E_ROW = 8
EPS = 0.05
MASK_SHARE = 0.3


def load_scale_rows(queue, plane, scales, first_row):
    rows = scales[0].bitcast(I32)
    for r in range(4):
        queue.dma_start(out=plane[:].bitcast(I32)[first_row + r : P : 32, :], in_=rows[r:16:4, :])


def tile_picked_ymaskn_tanh_p_kernel(
    tc, x_words, x_scales, e_words, e_scales, w1, w2_words, w2_scales, w3, offs, fea, out
):
    nc = tc.nc
    with ExitStack() as ctx:
        lists = ctx.enter_context(tc.tile_pool(name="lists", bufs=1))
        sb = ctx.enter_context(tc.tile_pool(name="sb", bufs=1))
        psum = ctx.enter_context(tc.psum_pool(name="psum", bufs=1))

        offs_sb = lists.tile([P, S // 16], U16, name="offs_sb")
        fea_sb = lists.tile([P, S // 16], U16, name="fea_sb")
        x_plane = sb.tile([P, T], U8, name="x_plane")
        e_plane = sb.tile([P, T], U8, name="e_plane", tag="w3_codes", align_bytes=64)
        w2_plane = sb.tile([P, N], U8, name="w2_plane", align_bytes=64)
        w2_codes = sb.tile([P, 2 * N], U8, name="w2_codes", align_bytes=64)
        x_table = sb.tile([P, T], U32, name="x_table")
        e_table = sb.tile([P, T], U32, name="e_table", tag="h_codes", align_bytes=64)
        w1_raw = [sb.tile([P, PACK, H // 2], F32, name="w1_raw%d" % c) for c in range(2)]
        w3_raw = sb.tile([P, PACK, N], F32, name="w3_raw", tag="h_bf0", align_bytes=64)
        power = sb.tile([P, 1], F32, name="power")

        nc.vector.memset(x_plane[:].bitcast(I32), 0)
        nc.vector.memset(e_plane[:].bitcast(I32), 0)
        nc.vector.memset(w2_plane[:].bitcast(I32), 0)
        nc.vector.memset(power[:], -0.5)

        w1_rows = w1.rearrange("(p j) c -> p j c", j=PACK)
        nc.sync.dma_start(offs_sb[:], offs)
        for c in range(2):
            nc.sync.dma_start(out=w1_raw[c][:], in_=w1_rows[:, :, c * H // 2 : (c + 1) * H // 2])
        load_scale_rows(nc.sync, x_plane, x_scales, X_ROW)
        nc.sync.dma_start(out=x_table[:].bitcast(I32), in_=x_words[0].rearrange("p n t -> p (n t)").bitcast(I32))
        nc.sync.dma_start(fea_sb[:], fea)
        nc.sync.dma_start(out=w3_raw[:], in_=w3.rearrange("(p j) c -> p j c", j=PACK))
        load_scale_rows(nc.sync, e_plane, e_scales, E_ROW)
        nc.sync.dma_start(out=e_table[:].bitcast(I32), in_=e_words[0].rearrange("p n t -> p (n t)").bitcast(I32))
        nc.sync.dma_start(out=w2_codes[:].bitcast(I32), in_=w2_words[0].bitcast(I32))
        load_scale_rows(nc.sync, w2_plane, w2_scales, 0)

        w1_bf = sb.tile([P, PACK, P, PACK], BF16, name="w1_bf", align_bytes=64)
        dealt = [w1_bf[:, :, c * P // 2 : (c + 1) * P // 2, :].rearrange("p t m j -> p m t j") for c in range(2)]
        plain = [w1_raw[c][:].rearrange("p j (m t) -> p m t j", t=PACK) for c in range(2)]
        nc.vector.tensor_copy(out=dealt[0], in_=plain[0])
        nc.scalar.activation(out=dealt[1], in_=plain[1], func=ACT.Copy)
        x_bytes = sb.tile([P, S], U8, name="x_bytes", align_bytes=64)
        nc.vector.tensor_copy(x_bytes[:], x_plane[:].indirect(offs_sb[:]))
        w1_codes = sb.tile([P, H], U32, name="w1_codes", align_bytes=64)
        w1_bytes = sb.tile([P, H], U8, name="w1_bytes", align_bytes=64)
        nc.vector.quantize_mx(
            out=w1_codes[:].bitcast(FP8X4), scales=w1_bytes[:], in_=w1_bf[:].rearrange("p t m j -> p (t m j)")
        )

        x_codes = [sb.tile([P, HALF], U32, name="x_codes%d" % h, align_bytes=64) for h in range(2)]
        for h in range(2):
            nc.vector.tensor_copy(x_codes[h][:], x_table[:].indirect(offs_sb[:, h * HALF // 16 : (h + 1) * HALF // 16]))

        e_bytes = sb.tile([P, S], U8, name="e_bytes", align_bytes=64)
        nc.vector.tensor_copy(e_bytes[:], e_plane[:].indirect(fea_sb[:]))
        w3_bf = sb.tile([P, N, PACK], BF16, name="w3_bf", align_bytes=64)
        nc.scalar.activation(
            out=w3_bf[:].rearrange("p (c i) j -> p c j i", i=4),
            in_=w3_raw[:].rearrange("p j (c i) -> p c j i", i=4),
            func=ACT.Copy,
        )
        w3_codes = sb.tile([P, N], U32, name="w3_codes", tag="w3_codes", align_bytes=64)
        w3_bytes = sb.tile([P, N], U8, name="w3_bytes", align_bytes=64)
        nc.vector.quantize_mx(
            out=w3_codes[:].bitcast(FP8X4), scales=w3_bytes[:], in_=w3_bf[:].rearrange("p c j -> p (c j)")
        )

        h_bf = sb.tile([P, S, PACK], BF16, name="h_bf", tag="h_bf0", align_bytes=64)
        for chunk in range(S // CHUNK):
            h, c = divmod(chunk, HALF // CHUNK)
            bank = psum.tile([P, PACK, CHUNK], F32, name="h_bank%d" % chunk)
            for t in range(PACK):
                nc.tensor.matmul_mx(
                    out=bank[:, t, :],
                    lhsT=w1_codes[:, t * P : (t + 1) * P].bitcast(FP8X4),
                    lhsT_scale=w1_bytes[:, t * P : (t + 1) * P],
                    rhs=x_codes[h][:, c * CHUNK : (c + 1) * CHUNK].bitcast(FP8X4),
                    rhs_scale=x_bytes[X_ROW:P, chunk * CHUNK : (chunk + 1) * CHUNK],
                    start=True,
                    stop=True,
                )
            woven = h_bf[:, chunk * CHUNK : (chunk + 1) * CHUNK, :]
            nc.scalar.activation(out=woven, in_=bank[:].rearrange("p t n -> p n t"), func=ACT.Relu)

        e_codes = [sb.tile([P, HALF], U32, name="e_codes%d" % h, align_bytes=64) for h in range(2)]
        f_banks = [psum.tile([P, HALF], F32, name="f_bank%d" % h) for h in range(2)]
        mask_banks = [psum.tile([P, HALF], F32, name="mask_bank%d" % h) for h in range(2)]
        for h in range(2):
            nc.vector.tensor_copy(e_codes[h][:], e_table[:].indirect(fea_sb[:, h * HALF // 16 : (h + 1) * HALF // 16]))
            nc.tensor.matmul_mx(
                out=f_banks[h][:],
                lhsT=w3_codes[:].bitcast(FP8X4),
                lhsT_scale=w3_bytes[:],
                rhs=e_codes[h][:].bitcast(FP8X4),
                rhs_scale=e_bytes[E_ROW:P, h * HALF : (h + 1) * HALF],
                start=True,
                stop=True,
            )
        h_codes = sb.tile([P, S], U32, name="h_codes", tag="h_codes", align_bytes=64)
        h_bytes = sb.tile([P, S], U8, name="h_bytes", align_bytes=64)
        nc.vector.quantize_mx(
            out=h_codes[:].bitcast(FP8X4), scales=h_bytes[:], in_=h_bf[:].rearrange("p n t -> p (n t)")
        )
        for h in range(2):
            nc.tensor.matmul_mx(
                out=mask_banks[h][:],
                lhsT=w2_codes[:].bitcast(FP4X4),
                lhsT_scale=w2_plane[:],
                rhs=h_codes[:, h * HALF : (h + 1) * HALF].bitcast(FP8X4),
                rhs_scale=h_bytes[:, h * HALF : (h + 1) * HALF],
                start=True,
                stop=True,
            )

        stats = sb.tile([P, 9], F32, name="stats")
        sums = sb.tile([P, 2], F32, name="sums")
        f_first = sb.tile([P, HALF], F32, name="f_first")
        squares = sb.tile([P, HALF], F32, name="squares")
        nc.vector.memset(stats[:, 0:1], float(HALF))
        nc.scalar.activation(out=f_first[:], in_=f_banks[0][:], func=ACT.Copy, accum_out=sums[:, 0:1])
        nc.scalar.activation(out=stats[:, 1:2], in_=sums[:, 0:1], func=ACT.Copy, scale=1.0 / HALF)
        nc.scalar.activation(
            out=squares[:], in_=f_first[:], func=ACT.Square, scale=-1.0, bias=stats[:, 1:2], accum_out=sums[:, 1:2]
        )
        nc.scalar.activation(out=stats[:, 2:3], in_=sums[:, 1:2], func=ACT.Copy, bias=EPS * S)
        nc.vector.bn_stats(out=stats[:, 3:9], in_=f_banks[1][:])
        moments = sb.tile([P, 2], F32, name="moments")
        nc.vector.bn_aggr(out=moments[:], in_=stats[:])
        gain = sb.tile([P, 1], F32, name="gain")
        nc.gpsimd.tensor_tensor(out=gain[:], in0=moments[:, 1:2], in1=power[:], op=ALU.pow)

        mask_second = sb.tile([P, HALF], F32, name="mask_second")
        nc.scalar.activation(out=mask_second[:], in_=mask_banks[1][:], func=ACT.Copy)
        factors = [(f_first, mask_banks[0]), (f_banks[1], mask_second)]
        prod = [sb.tile([P, HALF], F32, name="prod%d" % h) for h in range(2)]
        bounded = [sb.tile([P, HALF], F32, name="bounded%d" % h) for h in range(2)]
        result = [sb.tile([P, HALF], F32, name="result%d" % h) for h in range(2)]
        for h in range(2):
            nc.vector.scalar_tensor_tensor(
                out=prod[h][:], in0=factors[h][0][:], scalar=moments[:, 0:1], in1=factors[h][1][:],
                op0=ALU.subtract, op1=ALU.mult,
            )
            nc.scalar.activation(out=bounded[h][:], in_=prod[h][:], func=ACT.Tanh, scale=gain[:])
        for h in range(2):
            nc.vector.scalar_tensor_tensor(
                out=result[h][:], in0=mask_banks[h][:], scalar=MASK_SHARE, in1=bounded[h][:],
                op0=ALU.mult, op1=ALU.add,
            )
            nc.sync.dma_start(out=out[:, h * HALF : (h + 1) * HALF], in_=result[h][:])
